import numpy as np, ml_dtypes
CORES = [2,10,18,26,34,42,50,58,66,74,82,90,98,106,114,122]
N = 16
PERM = [[0,4],[1,5],[2,6],[3,7],[4,8],[5,9],[6,10],[7,11],[8,12],[9,13],[10,14],[11,15],[12,0],[13,1],[14,2],[15,3]]
def setup_inputs(rng):
    return {"x": rng.standard_normal((N, 128, 512), dtype=np.float32).astype(ml_dtypes.bfloat16)}
def reference(x):
    y = np.empty_like(x)
    for s, d in PERM:
        y[d] = x[s]
    return {"y": y}

@@ -1,0 +1,88 @@
+from concourse.bass import DstId, RemoteDMATransfer
+
+ROW_ELEMS = 512
+PIECES = [(32, None), (32, 6), (32, None), (32, 7)]
+CALLS = [[(1, 0xFF00), (0, 0x00FF)], [(3, 0xFF00), (2, 0x00FF)]]
+LOADQ = ["scalar", "sync", "scalar", "sync"]
+STOREQ = ["scalar", "sync", "scalar", "sync"]
+FWD_MASK = 0x00FF
+
+NP = len(PIECES)
+OFFS = [sum(p[0] for p in PIECES[:i]) for i in range(NP)]
+
+SCRATCH = {}
+for ip in range(NP):
+    ncol = PIECES[ip][0] * ROW_ELEMS // 128
+    SCRATCH["s%d" % ip] = ("dram", [128, ncol], "bfloat16")
+    SCRATCH["r%d" % ip] = ("dram", [128, ncol], "bfloat16")
+SEMAPHORES = ["ld%d" % c for c in range(len(CALLS))] + ["arr%d" % p for p in range(NP)] + ["snt", "st"]
+
+
+def nbits(m):
+    return bin(m).count("1")
+
+
+def queue(g, name):
+    if name == "sync":
+        return g.sync
+    if name == "scalar":
+        return g.scalar
+    return g
+
+
+def rank_program(g, core, T, topo):
+    perm = T.tables["PERM"]
+    cores = T.cores
+    rank = T.rank_of(core)
+    chip, k = core // 8, core % 8
+
+    if rank is None:
+        mine = [p for p in range(NP) if PIECES[p][1] == k]
+        owner = [r for r in range(len(cores)) if cores[r] // 8 == chip]
+        if not mine or not owner:
+            return
+        dst = cores[[d for s, d in perm if s == owner[0]][0]]
+        rid, pid, se = topo.addr(dst)
+        onchip = {p: m for call in CALLS for p, m in call}
+        sent = 0
+        for p in mine:
+            g.wait_ge(T.sem["arr%d" % p], nbits(onchip[p]))
+            g.remote_dma(T["r%d" % p][:], T["r%d" % p][:], T.sem["arr%d" % p], T.sem.snt, pid, rid, FWD_MASK)
+            sent += nbits(FWD_MASK)
+        g.wait_ge(T.sem.snt, sent)
+        return
+
+    dst = cores[[d for s, d in perm if s == rank][0]]
+
+    for c, call in enumerate(CALLS):
+        for p, m in call:
+            r0 = OFFS[p]
+            queue(g, LOADQ[p]).dma_start(T["s%d" % p][:], T.x[r0:r0 + PIECES[p][0], :]).then_inc(T.sem["ld%d" % c], 16)
+
+    for call in CALLS:
+        for p, m in call:
+            q = queue(g, STOREQ[p])
+            r0 = OFFS[p]
+            q.wait_ge(T.sem["arr%d" % p], nbits(m) if PIECES[p][1] is None else nbits(FWD_MASK))
+            q.dma_start(T.y[r0:r0 + PIECES[p][0], :], T["r%d" % p][:]).then_inc(T.sem.st, 16)
+
+    sent = 0
+    for c, call in enumerate(CALLS):
+        g.wait_ge(T.sem["ld%d" % c], 16 * len(call))
+        trs = []
+        for p, m in call:
+            to = dst if PIECES[p][1] is None else chip * 8 + PIECES[p][1]
+            rid, pid, se = topo.addr(to)
+            trs.append((p, m, rid, pid))
+            sent += nbits(m)
+        if len(trs) == 1:
+            p, m, rid, pid = trs[0]
+            g.remote_dma(T["r%d" % p][:], T["s%d" % p][:], T.sem["arr%d" % p], T.sem.snt, pid, rid, m)
+        else:
+            g.remote_dma_fused(
+                [RemoteDMATransfer(dst_ids=[DstId(rid=rid, pnc=pid)], dma_engine_mask=m,
+                                   remote_sem=T.sem["arr%d" % p], src=T["s%d" % p][:], dst=T["r%d" % p][:])
+                 for p, m, rid, pid in trs],
+                local_sem=T.sem.snt)
+    g.wait_ge(T.sem.snt, sent)
+    g.wait_ge(T.sem.st, 16 * NP)

@@ -1,10 +1,10 @@
 from concourse.bass import DstId, RemoteDMATransfer
 
 ROW_ELEMS = 512
-PIECES = [(32, None), (32, 6), (32, None), (32, 7)]
-CALLS = [[(1, 0xFF00), (0, 0x00FF)], [(3, 0xFF00), (2, 0x00FF)]]
-LOADQ = ["scalar", "sync", "scalar", "sync"]
-STOREQ = ["scalar", "sync", "scalar", "sync"]
+PIECES = [(64, None), (64, None)]
+CALLS = [[(0, 0x00FF)], [(1, 0x00FF)]]
+LOADQ = ["sync", "sync"]
+STOREQ = ["scalar", "sync"]
 FWD_MASK = 0x00FF
 
 NP = len(PIECES)

@@ -1,88 +1,43 @@
-from concourse.bass import DstId, RemoteDMATransfer
-
 ROW_ELEMS = 512
-PIECES = [(64, None), (64, None)]
-CALLS = [[(0, 0x00FF)], [(1, 0x00FF)]]
+PIECES = [64, 64]
 LOADQ = ["sync", "sync"]
 STOREQ = ["scalar", "sync"]
-FWD_MASK = 0x00FF
+MASK = 0x00FF
 
 NP = len(PIECES)
-OFFS = [sum(p[0] for p in PIECES[:i]) for i in range(NP)]
+OFFS = [sum(PIECES[:i]) for i in range(NP)]
 
 SCRATCH = {}
 for ip in range(NP):
-    ncol = PIECES[ip][0] * ROW_ELEMS // 128
+    ncol = PIECES[ip] * ROW_ELEMS // 128
     SCRATCH["s%d" % ip] = ("dram", [128, ncol], "bfloat16")
     SCRATCH["r%d" % ip] = ("dram", [128, ncol], "bfloat16")
-SEMAPHORES = ["ld%d" % c for c in range(len(CALLS))] + ["arr%d" % p for p in range(NP)] + ["snt", "st"]
-
-
-def nbits(m):
-    return bin(m).count("1")
+SEMAPHORES = ["ld%d" % p for p in range(NP)] + ["arr%d" % p for p in range(NP)] + ["snt", "st"]
 
 
 def queue(g, name):
-    if name == "sync":
-        return g.sync
-    if name == "scalar":
-        return g.scalar
-    return g
+    return g.sync if name == "sync" else g.scalar
 
 
 def rank_program(g, core, T, topo):
-    perm = T.tables["PERM"]
-    cores = T.cores
     rank = T.rank_of(core)
-    chip, k = core // 8, core % 8
-
     if rank is None:
-        mine = [p for p in range(NP) if PIECES[p][1] == k]
-        owner = [r for r in range(len(cores)) if cores[r] // 8 == chip]
-        if not mine or not owner:
-            return
-        dst = cores[[d for s, d in perm if s == owner[0]][0]]
-        rid, pid, se = topo.addr(dst)
-        onchip = {p: m for call in CALLS for p, m in call}
-        sent = 0
-        for p in mine:
-            g.wait_ge(T.sem["arr%d" % p], nbits(onchip[p]))
-            g.remote_dma(T["r%d" % p][:], T["r%d" % p][:], T.sem["arr%d" % p], T.sem.snt, pid, rid, FWD_MASK)
-            sent += nbits(FWD_MASK)
-        g.wait_ge(T.sem.snt, sent)
         return
+    dst = T.cores[[d for s, d in T.tables["PERM"] if s == rank][0]]
+    rid, pid, se = topo.addr(dst)
 
-    dst = cores[[d for s, d in perm if s == rank][0]]
+    for p in range(NP):
+        r0 = OFFS[p]
+        queue(g, LOADQ[p]).dma_start(T["s%d" % p][:], T.x[r0:r0 + PIECES[p], :]).then_inc(T.sem["ld%d" % p], 16)
 
-    for c, call in enumerate(CALLS):
-        for p, m in call:
-            r0 = OFFS[p]
-            queue(g, LOADQ[p]).dma_start(T["s%d" % p][:], T.x[r0:r0 + PIECES[p][0], :]).then_inc(T.sem["ld%d" % c], 16)
+    for p in range(NP):
+        q = queue(g, STOREQ[p])
+        r0 = OFFS[p]
+        q.wait_ge(T.sem["arr%d" % p], 8)
+        q.dma_start(T.y[r0:r0 + PIECES[p], :], T["r%d" % p][:]).then_inc(T.sem.st, 16)
 
-    for call in CALLS:
-        for p, m in call:
-            q = queue(g, STOREQ[p])
-            r0 = OFFS[p]
-            q.wait_ge(T.sem["arr%d" % p], nbits(m) if PIECES[p][1] is None else nbits(FWD_MASK))
-            q.dma_start(T.y[r0:r0 + PIECES[p][0], :], T["r%d" % p][:]).then_inc(T.sem.st, 16)
-
-    sent = 0
-    for c, call in enumerate(CALLS):
-        g.wait_ge(T.sem["ld%d" % c], 16 * len(call))
-        trs = []
-        for p, m in call:
-            to = dst if PIECES[p][1] is None else chip * 8 + PIECES[p][1]
-            rid, pid, se = topo.addr(to)
-            trs.append((p, m, rid, pid))
-            sent += nbits(m)
-        if len(trs) == 1:
-            p, m, rid, pid = trs[0]
-            g.remote_dma(T["r%d" % p][:], T["s%d" % p][:], T.sem["arr%d" % p], T.sem.snt, pid, rid, m)
-        else:
-            g.remote_dma_fused(
-                [RemoteDMATransfer(dst_ids=[DstId(rid=rid, pnc=pid)], dma_engine_mask=m,
-                                   remote_sem=T.sem["arr%d" % p], src=T["s%d" % p][:], dst=T["r%d" % p][:])
-                 for p, m, rid, pid in trs],
-                local_sem=T.sem.snt)
-    g.wait_ge(T.sem.snt, sent)
+    for p in range(NP):
+        g.wait_ge(T.sem["ld%d" % p], 16)
+        g.remote_dma(T["r%d" % p][:], T["s%d" % p][:], T.sem["arr%d" % p], T.sem.snt, pid, rid, MASK)
+    g.wait_ge(T.sem.snt, 8 * NP)
     g.wait_ge(T.sem.st, 16 * NP)

ROW_ELEMS = 512
PIECES = [64, 64]
LOADQ = ["sync", "sync"]
STOREQ = ["scalar", "sync"]
MASK = 0x00FF

NP = len(PIECES)
OFFS = [sum(PIECES[:i]) for i in range(NP)]

SCRATCH = {}
for ip in range(NP):
    ncol = PIECES[ip] * ROW_ELEMS // 128
    SCRATCH["s%d" % ip] = ("dram", [128, ncol], "bfloat16")
    SCRATCH["r%d" % ip] = ("dram", [128, ncol], "bfloat16")
SEMAPHORES = ["ld%d" % p for p in range(NP)] + ["arr%d" % p for p in range(NP)] + ["snt", "st"]


def queue(g, name):
    return g.sync if name == "sync" else g.scalar


def rank_program(g, core, T, topo):
    rank = T.rank_of(core)
    if rank is None:
        return
    dst = T.cores[[d for s, d in T.tables["PERM"] if s == rank][0]]
    rid, pid, se = topo.addr(dst)

    for p in range(NP):
        r0 = OFFS[p]
        queue(g, LOADQ[p]).dma_start(T["s%d" % p][:], T.x[r0:r0 + PIECES[p], :]).then_inc(T.sem["ld%d" % p], 16)

    for p in range(NP):
        q = queue(g, STOREQ[p])
        r0 = OFFS[p]
        q.wait_ge(T.sem["arr%d" % p], 8)
        q.dma_start(T.y[r0:r0 + PIECES[p], :], T["r%d" % p][:]).then_inc(T.sem.st, 16)

    for p in range(NP):
        g.wait_ge(T.sem["ld%d" % p], 16)
        g.remote_dma(T["r%d" % p][:], T["s%d" % p][:], T.sem["arr%d" % p], T.sem.snt, pid, rid, MASK)
    g.wait_ge(T.sem.snt, 8 * NP)
    g.wait_ge(T.sem.st, 16 * NP)
